import numpy as np
import ml_dtypes


def mxq(x, axis, fmt="e4m3"):
    dtype, down = {"e4m3": (ml_dtypes.float8_e4m3fn, 7), "e5m2": (ml_dtypes.float8_e5m2, 14)}[fmt]
    v = np.moveaxis(np.asarray(x, np.float32).astype(ml_dtypes.bfloat16).astype(np.float64), axis, -1)
    blocks = v.reshape(v.shape[:-1] + (-1, 32))
    amax = np.abs(blocks).max(-1, keepdims=True)
    byte = np.maximum(np.where(amax > 0, np.frexp(amax)[1] - 1 + 127, 0) - down, 1)
    scale = np.exp2(byte - 127.0)
    codes = (blocks / scale).astype(np.float32).astype(dtype).astype(np.float64)
    return np.moveaxis((codes * scale).reshape(v.shape), -1, axis)


WIDE = False


def mx_kscale(k):
    if not WIDE:
        return np.ones(k)
    levels = np.array([10, -10, 5, -5, 0])
    if k % 512:
        return np.exp2(np.random.permutation(np.resize(levels, k // 32))).repeat(32)
    a = np.empty((k // 512, 16))
    for p in range(k // 512):
        a[p, :8] = np.random.permutation(np.resize(levels, 8))
        for g in range(8):
            far = levels[np.abs(levels - a[p, g]) >= 10]
            a[p, g + 8] = far[np.random.randint(len(far))]
    return np.exp2(a.ravel()).repeat(32)


BF16 = ml_dtypes.bfloat16


def bf(x):
    return np.asarray(x, np.float32).astype(BF16)


def f64(x):
    return np.asarray(x).astype(np.float64)


E2M1 = np.array([0.0, 0.5, 1.0, 1.5, 2.0, 3.0, 4.0, 6.0, -0.0, -0.5, -1.0, -1.5, -2.0, -3.0, -4.0, -6.0])


def pack_weight(w, fmt):
    k, n = w.shape
    w = f64(bf(w)).reshape(k // 32, 32, n)
    amax = np.abs(w).max(1)
    if fmt == "e4m3":
        byte = np.frexp(amax)[1] - 1 + 127 - 7
    else:
        mant, ex = np.frexp(amax / 6.0)
        byte = np.where(mant > 0.5, ex, ex - 1) + 127
    byte = np.clip(np.where(amax > 0, byte, 1), 1, 254)
    scaled = (w * np.exp2(127.0 - byte)[:, None, :]).reshape(k, n).astype(np.float32)
    by_word = np.ascontiguousarray(scaled.reshape(k // 512, 128, 4, n).transpose(0, 1, 3, 2))
    if fmt == "e4m3":
        words = by_word.astype(ml_dtypes.float8_e4m3fn).view(np.uint8)
    else:
        c = by_word.astype(ml_dtypes.float4_e2m1fn).view(np.uint8) & 0xF
        words = c[..., 0::2] | (c[..., 1::2] << 4)
    return np.ascontiguousarray(words), np.ascontiguousarray(byte.astype(np.uint8).reshape(k // 512, 16, n))


def unpack_weight(words, scales, fmt):
    g, p, n, _ = words.shape
    if fmt == "e4m3":
        vals = np.ascontiguousarray(words).view(ml_dtypes.float8_e4m3fn).astype(np.float64)
    else:
        nib = np.empty((g, p, n, 4), np.uint8)
        nib[..., 0::2] = words & 0xF
        nib[..., 1::2] = words >> 4
        vals = E2M1[nib]
    vals = vals * np.repeat(np.exp2(scales.astype(np.float64) - 127.0), 8, axis=1)[..., None]
    return vals.transpose(0, 1, 3, 2).reshape(g * 512, n)
def pack4(w):
    words, scales = pack_weight(w, "e2m1")
    return words.reshape(words.shape[0], 128, -1), scales


def unpack4(words, scales):
    return unpack_weight(words.reshape(words.shape[0], 128, -1, 2), scales, "e2m1")


M, K, N = 1024, 1536, 1024


def setup_inputs():
    s = mx_kscale(K)
    amp = np.random.standard_normal((M, K)) * s
    res = np.exp(0.3 * np.random.standard_normal((M, K)))
    phi_words, phi_scales = pack4(np.random.standard_normal((K, N)) / np.sqrt(K) / s[:, None])
    grad_words, grad_scales = pack_weight(np.random.standard_normal((K, N)) / np.sqrt(K) / s[:, None], "e4m3")
    delta = 0.5 * np.random.standard_normal((K, N)) / np.sqrt(K) / s[:, None]
    pattern = 0.7 + 0.2 * np.random.standard_normal(N)
    return {"amp": bf(amp),
            "res": bf(res),
            "phi_words": phi_words,
            "phi_scales": phi_scales,
            "grad_words": grad_words,
            "grad_scales": grad_scales,
            "delta": bf(delta),
            "pattern": bf(pattern)}


def reference(amp, res, phi_words, phi_scales, grad_words, grad_scales, delta, pattern):
    x = mxq(f64(amp) * f64(res), 1, "e4m3")
    base = x @ unpack4(phi_words, phi_scales)
    corr = x @ mxq(f64(delta), 0, "e4m3")
    p = base + corr
    u = x @ unpack_weight(grad_words, grad_scales, "e4m3")
    signal = p + f64(pattern) * u
    intensity = p * u
    return signal, intensity

@@ -1,0 +1,331 @@
+from contextlib import ExitStack
+
+import concourse.mybir as mybir
+from concourse.masks import make_identity
+
+M, K, N = 1024, 1536, 1024
+FLOPS = 3 * 2 * M * K * N
+
+F32 = mybir.dt.float32
+BF16 = mybir.dt.bfloat16
+I32 = mybir.dt.int32
+U32 = mybir.dt.uint32
+U8 = mybir.dt.uint8
+FP8X4 = mybir.dt.float8_e4m3fn_x4
+FP4X4 = mybir.dt.float4_e2m1fn_x4
+MULT = mybir.AluOpType.mult
+ADD = mybir.AluOpType.add
+
+P = 128
+PACK = 4
+PASSES = K // (P * PACK)
+HALF = 512
+TILES = M // P
+PIECE = 128
+
+
+def tile_room_mode_microphones_s10_kernel(
+    tc, amp, res, phi_words, phi_scales, grad_words, grad_scales, delta, pattern, out_0, out_1
+):
+    nc = tc.nc
+    with ExitStack() as ctx:
+        keep = ctx.enter_context(tc.tile_pool(name="keep", bufs=1))
+        work = ctx.enter_context(tc.tile_pool(name="work", bufs=3))
+        psum = ctx.enter_context(tc.psum_pool(name="psum", bufs=1))
+        results = ctx.enter_context(tc.tile_pool(name="results", bufs=8))
+        ctx.enter_context(tc.manual_schedule())
+
+        ident = keep.tile([P, P], F32, name="ident")
+        make_identity(nc, ident[:])
+
+        phi_plane = keep.tile([P, PASSES, N], U8, name="phi_plane", align_bytes=64)
+        grad_plane = keep.tile([P, PASSES, N], U8, name="grad_plane", align_bytes=64)
+        for plane in (phi_plane, grad_plane):
+            nc.vector.memset(plane[:].rearrange("p g n -> p (g n)").bitcast(I32), 0)
+
+        def load_scales(plane, rows):
+            by_row = rows.rearrange("g (q r) n -> r q g n", r=4)
+            for r in range(4):
+                nc.sync.dma_start(out=plane[r:P:32, :, :].bitcast(I32), in_=by_row[r].bitcast(I32))
+
+        amp_sb, res_sb, phi_sb, grad_sb, delta_sb = {}, {}, {}, {}, {}
+
+        def load_x(i):
+            amp_sb[i] = keep.tile([P, K], BF16, name="amp%d" % i)
+            res_sb[i] = keep.tile([P, K], BF16, name="res%d" % i)
+            nc.sync.dma_start(out=amp_sb[i][:], in_=amp[i * P : (i + 1) * P, :])
+            nc.sync.dma_start(out=res_sb[i][:], in_=res[i * P : (i + 1) * P, :])
+
+        def load_phi(h):
+            phi_sb[h] = keep.tile([P, PASSES, 2 * HALF], U8, name="phi%d" % h, align_bytes=64)
+            src = phi_words.rearrange("g p b -> p g b")[:, :, 2 * HALF * h : 2 * HALF * (h + 1)]
+            nc.sync.dma_start(out=phi_sb[h][:].bitcast(I32), in_=src.bitcast(I32))
+
+        def load_grad(h):
+            for g in range(PASSES):
+                grad_sb[h, g] = keep.tile([P, HALF], U32, name="grad%d%d" % (h, g), align_bytes=64)
+                src = grad_words[g].rearrange("p n t -> p (n t)")[:, PACK * HALF * h : PACK * HALF * (h + 1)]
+                nc.sync.dma_start(out=grad_sb[h, g][:].bitcast(I32), in_=src.bitcast(I32))
+
+        def load_delta(h):
+            for g in range(PASSES):
+                delta_sb[h, g] = keep.tile([P, PACK, HALF], BF16, name="delta%d%d" % (h, g))
+                rows = delta[P * PACK * g : P * PACK * (g + 1), HALF * h : HALF * (h + 1)]
+                nc.sync.dma_start(out=delta_sb[h, g][:], in_=rows.rearrange("(p t) n -> p t n", t=PACK))
+
+        pattern_rows = keep.tile([P, N // P], BF16, name="pattern_rows")
+        nc.sync.dma_start(out=pattern_rows[:], in_=pattern.rearrange("(p c) -> p c", p=P))
+        load_x(0)
+        load_scales(phi_plane, phi_scales)
+        load_x(1)
+        load_phi(0)
+        load_scales(grad_plane, grad_scales)
+        load_grad(0)
+        load_x(2)
+        load_grad(1)
+        load_delta(0)
+        load_phi(1)
+        load_x(3)
+        load_x(4)
+        load_delta(1)
+        for i in range(5, TILES):
+            load_x(i)
+
+        pattern_sb = keep.tile([P, N], BF16, name="pattern_sb")
+        pattern_words = pattern_rows[:].bitcast(F32)
+        spread = psum.tile([P, 4, P], F32, name="spread", tag="turn_a")
+        for c in range(4):
+            nc.tensor.transpose(spread[:, c, :], pattern_words[:, c : c + 1].to_broadcast([P, P]), ident[:])
+        nc.scalar.copy(
+            out=pattern_sb[:].bitcast(F32).rearrange("q (p c) -> q p c", c=4),
+            in_=spread[:].rearrange("q c p -> q p c"),
+        )
+
+        x_sorted, x_codes, x_plane, d_codes, d_plane = {}, {}, {}, {}, {}
+        x_grouped, d_grouped, u_sb, p_bank, weighted = {}, {}, {}, {}, {}
+        free_banks = list(range(6))
+
+        def multiply(i):
+            x_sorted[i] = work.tile([P, K], BF16, name="x_sorted")
+            nc.vector.tensor_tensor(
+                out=x_sorted[i][:].rearrange("m (u w e) -> m u w e", u=2, e=2),
+                in0=amp_sb[i][:].rearrange("m (w u e) -> m u w e", u=2, e=2),
+                in1=res_sb[i][:].rearrange("m (w u e) -> m u w e", u=2, e=2),
+                op=MULT,
+            )
+
+        def turn(i):
+            words = x_sorted[i][:].bitcast(F32)
+            bank_a = psum.tile([P, 4, P], F32, name="bank_a", tag="turn_a")
+            bank_b = psum.tile([P, 2, P], F32, name="bank_b", tag="turn_b")
+            for g in range(PASSES):
+                for u in range(2):
+                    dst = bank_a[:, 2 * g + u, :] if g < 2 else bank_b[:, u, :]
+                    first = u * (K // 4) + g * P
+                    nc.tensor.transpose(dst, words[:, first : first + P], ident[:])
+            grouped_a = work.tile([P, 1024], BF16, name="grouped_a", align_bytes=64)
+            grouped_b = work.tile([P, 512], BF16, name="grouped_b", align_bytes=64)
+            nc.scalar.copy(
+                out=grouped_a[:].bitcast(F32).rearrange("p (g m u) -> p g m u", g=2, u=2),
+                in_=bank_a[:].rearrange("p (g u) m -> p g m u", g=2),
+            )
+            nc.scalar.copy(
+                out=grouped_b[:].bitcast(F32).rearrange("p (m u) -> p m u", u=2),
+                in_=bank_b[:].rearrange("p u m -> p m u"),
+            )
+            x_grouped[i] = (grouped_a, grouped_b)
+
+        def quantize_x(i):
+            grouped_a, grouped_b = x_grouped[i]
+            x_codes[i] = keep.tile([P, PASSES * P], U32, name="x_codes%d" % i, align_bytes=64)
+            x_plane[i] = keep.tile([P, PASSES * P], U8, name="x_plane%d" % i, align_bytes=64)
+            nc.vector.quantize_mx(
+                out=x_codes[i][:, : 2 * P].bitcast(FP8X4), scales=x_plane[i][:, : 2 * P], in_=grouped_a[:]
+            )
+            nc.vector.quantize_mx(
+                out=x_codes[i][:, 2 * P :].bitcast(FP8X4), scales=x_plane[i][:, 2 * P :], in_=grouped_b[:]
+            )
+
+        def regroup(h, g, first, last, on_vector):
+            if (h, g) not in d_grouped:
+                d_grouped[h, g] = work.tile([P, HALF * PACK], BF16, name="delta_grouped", align_bytes=64)
+            dst = d_grouped[h, g][:, PACK * PIECE * first : PACK * PIECE * last]
+            src = delta_sb[h, g][:, :, PIECE * first : PIECE * last]
+            dst = dst.rearrange("p (c i t) -> p c t i", i=4, t=PACK)
+            src = src.rearrange("p t (c i) -> p c t i", i=4)
+            if on_vector:
+                nc.vector.tensor_copy(out=dst, in_=src)
+            else:
+                nc.scalar.copy(out=dst, in_=src)
+
+        def quantize_delta(h, g):
+            d_codes[h, g] = keep.tile([P, HALF], U32, name="d_codes%d%d" % (h, g), align_bytes=64)
+            d_plane[h, g] = keep.tile([P, HALF], U8, name="d_plane%d%d" % (h, g), align_bytes=64)
+            nc.vector.quantize_mx(out=d_codes[h, g][:].bitcast(FP8X4), scales=d_plane[h, g][:], in_=d_grouped[h, g][:])
+
+        def mx_pass(bank, i, g, rhs, rhs_scale, start, stop):
+            nc.tensor.matmul_mx(
+                out=bank[:],
+                lhsT=x_codes[i][:, g * P : (g + 1) * P].bitcast(FP8X4),
+                lhsT_scale=x_plane[i][:, g * P : (g + 1) * P],
+                rhs=rhs,
+                rhs_scale=rhs_scale,
+                start=start,
+                stop=stop,
+            )
+
+        def velocity(i, h):
+            number = free_banks.pop(0)
+            bank = psum.tile([P, HALF], F32, name="sum%d" % number)
+            for g in range(PASSES):
+                scale = grad_plane[:, g, HALF * h : HALF * (h + 1)]
+                mx_pass(bank, i, g, grad_sb[h, g][:].bitcast(FP8X4), scale, g == 0, g == PASSES - 1)
+            u_sb[i, h] = results.tile([P, HALF], F32, name="u_sb")
+            nc.scalar.copy(out=u_sb[i, h][:], in_=bank[:])
+            free_banks.append(number)
+
+        def base(i, h):
+            number = free_banks.pop(0)
+            bank = psum.tile([P, HALF], F32, name="sum%d" % number)
+            p_bank[i, h] = (number, bank)
+            for g in range(PASSES):
+                scale = phi_plane[:, g, HALF * h : HALF * (h + 1)]
+                mx_pass(bank, i, g, phi_sb[h][:, g, :].bitcast(FP4X4), scale, g == 0, False)
+
+        def correction(tiles, h, passes):
+            for g in passes:
+                for i in tiles:
+                    rhs = d_codes[h, g][:].bitcast(FP8X4)
+                    mx_pass(p_bank[i, h][1], i, g, rhs, d_plane[h, g][:], False, g == PASSES - 1)
+
+        def weigh(i, h):
+            weighted[i, h] = results.tile([P, HALF], F32, name="signal")
+            nc.vector.tensor_tensor(
+                out=weighted[i, h][:], in0=u_sb[i, h][:], in1=pattern_sb[:, HALF * h : HALF * (h + 1)], op=MULT
+            )
+
+        def finish(i, h):
+            cols = slice(HALF * h, HALF * (h + 1))
+            rows = slice(P * i, P * (i + 1))
+            number, bank = p_bank[i, h]
+            intensity = results.tile([P, HALF], F32, name="intensity")
+            signal = weighted[i, h]
+            nc.vector.tensor_tensor(out=intensity[:], in0=bank[:], in1=u_sb[i, h][:], op=MULT)
+            nc.vector.tensor_tensor(out=signal[:], in0=bank[:], in1=signal[:], op=ADD)
+            free_banks.append(number)
+            nc.sync.dma_start(out=out_1[rows, cols], in_=intensity[:])
+            nc.sync.dma_start(out=out_0[rows, cols], in_=signal[:])
+
+        def pressure(i, h):
+            base(i, h)
+            correction([i], h, range(PASSES))
+
+        multiply(0)
+        turn(0)
+        multiply(1)
+        quantize_x(0)
+        turn(1)
+        base(0, 0)
+        quantize_x(1)
+        velocity(0, 0)
+        multiply(2)
+        base(1, 0)
+        weigh(0, 0)
+        velocity(1, 0)
+        turn(2)
+        regroup(0, 0, 0, 3, True)
+        velocity(0, 1)
+        quantize_x(2)
+        regroup(0, 1, 3, 4, False)
+        regroup(0, 0, 3, 4, True)
+        velocity(1, 1)
+        quantize_delta(0, 0)
+        base(2, 0)
+        regroup(0, 1, 0, 3, True)
+        regroup(0, 2, 2, 4, False)
+        quantize_delta(0, 1)
+        regroup(0, 2, 0, 2, True)
+        velocity(2, 0)
+        velocity(2, 1)
+        quantize_delta(0, 2)
+        correction(range(3), 0, range(PASSES))
+        multiply(3)
+        finish(0, 0)
+        base(0, 1)
+        turn(3)
+        multiply(4)
+        weigh(1, 0)
+        base(1, 1)
+        base(2, 1)
+        quantize_x(3)
+        finish(1, 0)
+        weigh(2, 0)
+        regroup(1, 0, 0, 4, False)
+        velocity(3, 0)
+        turn(4)
+        finish(2, 0)
+        quantize_delta(1, 0)
+        pressure(3, 0)
+        weigh(3, 0)
+        quantize_x(4)
+        regroup(1, 1, 0, 2, False)
+        velocity(3, 1)
+        multiply(5)
+        finish(3, 0)
+        regroup(1, 1, 2, 4, False)
+        velocity(4, 0)
+        quantize_delta(1, 1)
+        pressure(4, 0)
+        weigh(4, 0)
+        regroup(1, 2, 0, 2, False)
+        velocity(4, 1)
+        finish(4, 0)
+        regroup(1, 2, 2, 4, False)
+        turn(5)
+        weigh(0, 1)
+        quantize_delta(1, 2)
+        correction(range(3), 1, range(2))
+        quantize_x(5)
+        base(3, 1)
+        correction(range(3), 1, [2])
+        correction([3], 1, range(PASSES))
+        finish(0, 1)
+        multiply(6)
+        velocity(5, 0)
+        weigh(1, 1)
+        finish(1, 1)
+        pressure(4, 1)
+        weigh(2, 1)
+        finish(2, 1)
+        turn(6)
+        weigh(3, 1)
+        finish(3, 1)
+        quantize_x(6)
+        multiply(7)
+        pressure(5, 0)
+        weigh(4, 1)
+        finish(4, 1)
+        velocity(5, 1)
+        weigh(5, 0)
+        finish(5, 0)
+        pressure(5, 1)
+        turn(7)
+        weigh(5, 1)
+        velocity(6, 0)
+        finish(5, 1)
+        quantize_x(7)
+        weigh(6, 0)
+        pressure(6, 0)
+        finish(6, 0)
+        velocity(6, 1)
+        weigh(6, 1)
+        pressure(6, 1)
+        finish(6, 1)
+        velocity(7, 0)
+        weigh(7, 0)
+        pressure(7, 0)
+        finish(7, 0)
+        velocity(7, 1)
+        weigh(7, 1)
+        pressure(7, 1)
+        finish(7, 1)

@@ -46,7 +46,7 @@ def tile_room_mode_microphones_s10_kernel(
         def load_scales(plane, rows):
             by_row = rows.rearrange("g (q r) n -> r q g n", r=4)
             for r in range(4):
-                nc.sync.dma_start(out=plane[r:P:32, :, :].bitcast(I32), in_=by_row[r].bitcast(I32))
+                nc.gpsimd.dma_start(out=plane[r:P:32, :, :].bitcast(I32), in_=by_row[r].bitcast(I32))
 
         amp_sb, res_sb, phi_sb, grad_sb, delta_sb = {}, {}, {}, {}, {}
 
@@ -75,21 +75,22 @@ def tile_room_mode_microphones_s10_kernel(
 
         pattern_rows = keep.tile([P, N // P], BF16, name="pattern_rows")
         nc.sync.dma_start(out=pattern_rows[:], in_=pattern.rearrange("(p c) -> p c", p=P))
-        load_x(0)
         load_scales(phi_plane, phi_scales)
+        load_scales(grad_plane, grad_scales)
+        load_x(0)
         load_x(1)
         load_phi(0)
-        load_scales(grad_plane, grad_scales)
         load_grad(0)
         load_x(2)
         load_grad(1)
-        load_delta(0)
-        load_phi(1)
         load_x(3)
+        load_delta(0)
         load_x(4)
+        load_x(5)
         load_delta(1)
-        for i in range(5, TILES):
-            load_x(i)
+        load_x(6)
+        load_x(7)
+        load_phi(1)
 
         pattern_sb = keep.tile([P, N], BF16, name="pattern_sb")
         pattern_words = pattern_rows[:].bitcast(F32)
@@ -180,7 +181,10 @@ def tile_room_mode_microphones_s10_kernel(
             for g in range(PASSES):
                 scale = grad_plane[:, g, HALF * h : HALF * (h + 1)]
                 mx_pass(bank, i, g, grad_sb[h, g][:].bitcast(FP8X4), scale, g == 0, g == PASSES - 1)
-            u_sb[i, h] = results.tile([P, HALF], F32, name="u_sb")
+            if h == 0:
+                u_sb[i, h] = results.tile([P, HALF], F32, name="u_first", bufs=5)
+            else:
+                u_sb[i, h] = results.tile([P, HALF], F32, name="u_second")
             nc.scalar.copy(out=u_sb[i, h][:], in_=bank[:])
             free_banks.append(number)
 
@@ -220,6 +224,31 @@ def tile_room_mode_microphones_s10_kernel(
             base(i, h)
             correction([i], h, range(PASSES))
 
+        def last_pressure(i, h):
+            rows = slice(P * i, P * (i + 1))
+            intensity = results.tile([P, HALF], F32, name="intensity")
+            signal = weighted[i, h]
+            for j in range(HALF // P):
+                part = slice(P * j, P * (j + 1))
+                number = free_banks.pop(0)
+                bank = psum.tile([P, P], F32, name="sum%d" % number)
+                for g in range(PASSES):
+                    scale = phi_plane[:, g, HALF * h + P * j : HALF * h + P * (j + 1)]
+                    rhs = phi_sb[h][:, g, 2 * P * j : 2 * P * (j + 1)].bitcast(FP4X4)
+                    mx_pass(bank, i, g, rhs, scale, g == 0, False)
+                for g in range(PASSES):
+                    rhs = d_codes[h, g][:, part].bitcast(FP8X4)
+                    mx_pass(bank, i, g, rhs, d_plane[h, g][:, part], False, g == PASSES - 1)
+                nc.vector.tensor_tensor(out=intensity[:, part], in0=bank[:], in1=u_sb[i, h][:, part], op=MULT)
+                nc.vector.tensor_tensor(out=signal[:, part], in0=bank[:], in1=signal[:, part], op=ADD)
+                free_banks.append(number)
+                if j >= 2:
+                    first = 0 if j == 2 else P * j
+                    done = slice(first, P * (j + 1))
+                    cols = slice(HALF * h + first, HALF * h + P * (j + 1))
+                    nc.sync.dma_start(out=out_1[rows, cols], in_=intensity[:, done])
+                    nc.sync.dma_start(out=out_0[rows, cols], in_=signal[:, done])
+
         multiply(0)
         turn(0)
         multiply(1)
@@ -233,99 +262,61 @@ def tile_room_mode_microphones_s10_kernel(
         weigh(0, 0)
         velocity(1, 0)
         turn(2)
-        regroup(0, 0, 0, 3, True)
         velocity(0, 1)
         quantize_x(2)
-        regroup(0, 1, 3, 4, False)
-        regroup(0, 0, 3, 4, True)
-        velocity(1, 1)
-        quantize_delta(0, 0)
-        base(2, 0)
-        regroup(0, 1, 0, 3, True)
-        regroup(0, 2, 2, 4, False)
-        quantize_delta(0, 1)
-        regroup(0, 2, 0, 2, True)
-        velocity(2, 0)
-        velocity(2, 1)
-        quantize_delta(0, 2)
-        correction(range(3), 0, range(PASSES))
         multiply(3)
-        finish(0, 0)
-        base(0, 1)
+        velocity(1, 1)
+        base(2, 0)
         turn(3)
-        multiply(4)
-        weigh(1, 0)
-        base(1, 1)
-        base(2, 1)
+        regroup(0, 0, 0, 4, True)
+        quantize_delta(0, 0)
+        regroup(0, 1, 3, 4, False)
+        velocity(2, 0)
         quantize_x(3)
-        finish(1, 0)
-        weigh(2, 0)
-        regroup(1, 0, 0, 4, False)
+        regroup(0, 1, 0, 3, True)
+        regroup(0, 2, 3, 4, False)
+        velocity(2, 1)
+        regroup(0, 2, 2, 3, False)
+        regroup(0, 2, 0, 2, True)
+        quantize_delta(0, 1)
         velocity(3, 0)
-        turn(4)
-        finish(2, 0)
-        quantize_delta(1, 0)
-        pressure(3, 0)
-        weigh(3, 0)
-        quantize_x(4)
-        regroup(1, 1, 0, 2, False)
+        quantize_delta(0, 2)
+        multiply(4)
+        base(3, 0)
         velocity(3, 1)
+        weigh(1, 0)
+        correction([0], 0, range(PASSES))
+        finish(0, 0)
+        correction([1], 0, range(PASSES))
+        turn(4)
+        regroup(1, 0, 0, 4, False)
         multiply(5)
-        finish(3, 0)
-        regroup(1, 1, 2, 4, False)
-        velocity(4, 0)
-        quantize_delta(1, 1)
-        pressure(4, 0)
-        weigh(4, 0)
-        regroup(1, 2, 0, 2, False)
-        velocity(4, 1)
-        finish(4, 0)
-        regroup(1, 2, 2, 4, False)
-        turn(5)
+        quantize_x(4)
+        finish(1, 0)
+        correction([2], 0, range(PASSES))
+        correction([3], 0, range(PASSES))
+        weigh(2, 0)
+        finish(2, 0)
+        weigh(3, 0)
+        for i in range(4, TILES):
+            step = i - 4
+            velocity(i, 0)
+            if i + 1 < TILES:
+                turn(i + 1)
+                quantize_x(i + 1)
+            if i + 2 < TILES:
+                multiply(i + 2)
+            regroup(1, 1 + step // 2, 2 * (step % 2), 2 * (step % 2) + 2, False)
+            finish(i - 1, 0)
+            weigh(i, 0)
+            if step > 0:
+                quantize_delta(1, step - 1)
+            pressure(i, 0)
+            velocity(i, 1)
+        finish(TILES - 1, 0)
         weigh(0, 1)
-        quantize_delta(1, 2)
-        correction(range(3), 1, range(2))
-        quantize_x(5)
-        base(3, 1)
-        correction(range(3), 1, [2])
-        correction([3], 1, range(PASSES))
-        finish(0, 1)
-        multiply(6)
-        velocity(5, 0)
-        weigh(1, 1)
-        finish(1, 1)
-        pressure(4, 1)
-        weigh(2, 1)
-        finish(2, 1)
-        turn(6)
-        weigh(3, 1)
-        finish(3, 1)
-        quantize_x(6)
-        multiply(7)
-        pressure(5, 0)
-        weigh(4, 1)
-        finish(4, 1)
-        velocity(5, 1)
-        weigh(5, 0)
-        finish(5, 0)
-        pressure(5, 1)
-        turn(7)
-        weigh(5, 1)
-        velocity(6, 0)
-        finish(5, 1)
-        quantize_x(7)
-        weigh(6, 0)
-        pressure(6, 0)
-        finish(6, 0)
-        velocity(6, 1)
-        weigh(6, 1)
-        pressure(6, 1)
-        finish(6, 1)
-        velocity(7, 0)
-        weigh(7, 0)
-        pressure(7, 0)
-        finish(7, 0)
-        velocity(7, 1)
-        weigh(7, 1)
-        pressure(7, 1)
-        finish(7, 1)
+        for i in range(TILES - 1):
+            pressure(i, 1)
+            weigh(i + 1, 1)
+            finish(i, 1)
+        last_pressure(TILES - 1, 1)

@@ -38,15 +38,15 @@ def tile_room_mode_microphones_s10_kernel(
         ident = keep.tile([P, P], F32, name="ident")
         make_identity(nc, ident[:])
 
-        phi_plane = keep.tile([P, PASSES, N], U8, name="phi_plane", align_bytes=64)
+        phi_plane = [keep.tile([P, PASSES, HALF], U8, name="phi_plane%d" % h, align_bytes=64) for h in range(2)]
         grad_plane = keep.tile([P, PASSES, N], U8, name="grad_plane", align_bytes=64)
-        for plane in (phi_plane, grad_plane):
+        for plane in (phi_plane[0], grad_plane, phi_plane[1]):
             nc.vector.memset(plane[:].rearrange("p g n -> p (g n)").bitcast(I32), 0)
 
-        def load_scales(plane, rows):
+        def load_scales(plane, rows, cols):
             by_row = rows.rearrange("g (q r) n -> r q g n", r=4)
             for r in range(4):
-                nc.gpsimd.dma_start(out=plane[r:P:32, :, :].bitcast(I32), in_=by_row[r].bitcast(I32))
+                nc.sync.dma_start(out=plane[r:P:32, :, :].bitcast(I32), in_=by_row[r][:, :, cols].bitcast(I32))
 
         amp_sb, res_sb, phi_sb, grad_sb, delta_sb = {}, {}, {}, {}, {}
 
@@ -67,29 +67,33 @@ def tile_room_mode_microphones_s10_kernel(
                 src = grad_words[g].rearrange("p n t -> p (n t)")[:, PACK * HALF * h : PACK * HALF * (h + 1)]
                 nc.sync.dma_start(out=grad_sb[h, g][:].bitcast(I32), in_=src.bitcast(I32))
 
-        def load_delta(h):
-            for g in range(PASSES):
-                delta_sb[h, g] = keep.tile([P, PACK, HALF], BF16, name="delta%d%d" % (h, g))
-                rows = delta[P * PACK * g : P * PACK * (g + 1), HALF * h : HALF * (h + 1)]
-                nc.sync.dma_start(out=delta_sb[h, g][:], in_=rows.rearrange("(p t) n -> p t n", t=PACK))
+        def load_delta(h, g):
+            delta_sb[h, g] = keep.tile([P, PACK, HALF], BF16, name="delta%d%d" % (h, g))
+            rows = delta[P * PACK * g : P * PACK * (g + 1), HALF * h : HALF * (h + 1)]
+            nc.sync.dma_start(out=delta_sb[h, g][:], in_=rows.rearrange("(p t) n -> p t n", t=PACK))
 
         pattern_rows = keep.tile([P, N // P], BF16, name="pattern_rows")
         nc.sync.dma_start(out=pattern_rows[:], in_=pattern.rearrange("(p c) -> p c", p=P))
-        load_scales(phi_plane, phi_scales)
-        load_scales(grad_plane, grad_scales)
         load_x(0)
         load_x(1)
+        load_scales(phi_plane[0], phi_scales, slice(0, HALF))
         load_phi(0)
-        load_grad(0)
         load_x(2)
-        load_grad(1)
+        load_scales(grad_plane, grad_scales, slice(0, N))
+        load_grad(0)
         load_x(3)
-        load_delta(0)
+        load_grad(1)
+        load_delta(0, 0)
+        load_delta(0, 1)
         load_x(4)
+        load_delta(0, 2)
         load_x(5)
-        load_delta(1)
+        load_delta(1, 0)
         load_x(6)
+        load_delta(1, 1)
         load_x(7)
+        load_delta(1, 2)
+        load_scales(phi_plane[1], phi_scales, slice(HALF, N))
         load_phi(1)
 
         pattern_sb = keep.tile([P, N], BF16, name="pattern_sb")
@@ -193,7 +197,7 @@ def tile_room_mode_microphones_s10_kernel(
             bank = psum.tile([P, HALF], F32, name="sum%d" % number)
             p_bank[i, h] = (number, bank)
             for g in range(PASSES):
-                scale = phi_plane[:, g, HALF * h : HALF * (h + 1)]
+                scale = phi_plane[h][:, g, :]
                 mx_pass(bank, i, g, phi_sb[h][:, g, :].bitcast(FP4X4), scale, g == 0, False)
 
         def correction(tiles, h, passes):
@@ -203,8 +207,9 @@ def tile_room_mode_microphones_s10_kernel(
                     mx_pass(p_bank[i, h][1], i, g, rhs, d_plane[h, g][:], False, g == PASSES - 1)
 
         def weigh(i, h):
-            weighted[i, h] = results.tile([P, HALF], F32, name="signal")
-            nc.vector.tensor_tensor(
+            weighted[i, h] = results.tile([P, HALF], F32, name="signal", bufs=5)
+            engine = nc.vector if h == 0 else nc.gpsimd
+            engine.tensor_tensor(
                 out=weighted[i, h][:], in0=u_sb[i, h][:], in1=pattern_sb[:, HALF * h : HALF * (h + 1)], op=MULT
             )
 
@@ -233,7 +238,7 @@ def tile_room_mode_microphones_s10_kernel(
                 number = free_banks.pop(0)
                 bank = psum.tile([P, P], F32, name="sum%d" % number)
                 for g in range(PASSES):
-                    scale = phi_plane[:, g, HALF * h + P * j : HALF * h + P * (j + 1)]
+                    scale = phi_plane[h][:, g, part]
                     rhs = phi_sb[h][:, g, 2 * P * j : 2 * P * (j + 1)].bitcast(FP4X4)
                     mx_pass(bank, i, g, rhs, scale, g == 0, False)
                 for g in range(PASSES):
@@ -256,48 +261,44 @@ def tile_room_mode_microphones_s10_kernel(
         turn(1)
         base(0, 0)
         quantize_x(1)
-        velocity(0, 0)
         multiply(2)
         base(1, 0)
-        weigh(0, 0)
-        velocity(1, 0)
         turn(2)
-        velocity(0, 1)
+        velocity(0, 0)
         quantize_x(2)
+        velocity(1, 0)
         multiply(3)
-        velocity(1, 1)
         base(2, 0)
-        turn(3)
-        regroup(0, 0, 0, 4, True)
-        quantize_delta(0, 0)
-        regroup(0, 1, 3, 4, False)
+        weigh(0, 0)
         velocity(2, 0)
+        turn(3)
+        weigh(1, 0)
+        weigh(2, 0)
+        velocity(0, 1)
         quantize_x(3)
-        regroup(0, 1, 0, 3, True)
-        regroup(0, 2, 3, 4, False)
+        velocity(1, 1)
+        regroup(0, 0, 0, 4, True)
+        regroup(0, 1, 3, 4, False)
         velocity(2, 1)
-        regroup(0, 2, 2, 3, False)
-        regroup(0, 2, 0, 2, True)
+        regroup(0, 1, 0, 3, True)
+        quantize_delta(0, 0)
+        base(3, 0)
+        multiply(4)
         quantize_delta(0, 1)
         velocity(3, 0)
-        quantize_delta(0, 2)
-        multiply(4)
-        base(3, 0)
+        regroup(0, 2, 3, 4, False)
+        regroup(0, 2, 0, 3, True)
         velocity(3, 1)
-        weigh(1, 0)
-        correction([0], 0, range(PASSES))
-        finish(0, 0)
-        correction([1], 0, range(PASSES))
+        quantize_delta(0, 2)
+        correction(range(4), 0, [0])
         turn(4)
-        regroup(1, 0, 0, 4, False)
-        multiply(5)
         quantize_x(4)
+        multiply(5)
+        correction(range(4), 0, [1, 2])
+        finish(0, 0)
+        regroup(1, 0, 0, 3, False)
         finish(1, 0)
-        correction([2], 0, range(PASSES))
-        correction([3], 0, range(PASSES))
-        weigh(2, 0)
         finish(2, 0)
-        weigh(3, 0)
         for i in range(4, TILES):
             step = i - 4
             velocity(i, 0)
@@ -306,11 +307,14 @@ def tile_room_mode_microphones_s10_kernel(
                 quantize_x(i + 1)
             if i + 2 < TILES:
                 multiply(i + 2)
+            if step == 0:
+                regroup(1, 0, 3, 4, False)
+                weigh(3, 0)
             regroup(1, 1 + step // 2, 2 * (step % 2), 2 * (step % 2) + 2, False)
-            finish(i - 1, 0)
-            weigh(i, 0)
             if step > 0:
                 quantize_delta(1, step - 1)
+            finish(i - 1, 0)
+            weigh(i, 0)
             pressure(i, 0)
             velocity(i, 1)
         finish(TILES - 1, 0)

from contextlib import ExitStack

import concourse.mybir as mybir
from concourse.masks import make_identity

M, K, N = 1024, 1536, 1024
FLOPS = 3 * 2 * M * K * N

F32 = mybir.dt.float32
BF16 = mybir.dt.bfloat16
I32 = mybir.dt.int32
U32 = mybir.dt.uint32
U8 = mybir.dt.uint8
FP8X4 = mybir.dt.float8_e4m3fn_x4
FP4X4 = mybir.dt.float4_e2m1fn_x4
MULT = mybir.AluOpType.mult
ADD = mybir.AluOpType.add

P = 128
PACK = 4
PASSES = K // (P * PACK)
HALF = 512
TILES = M // P
PIECE = 128


def tile_room_mode_microphones_s10_kernel(
    tc, amp, res, phi_words, phi_scales, grad_words, grad_scales, delta, pattern, out_0, out_1
):
    nc = tc.nc
    with ExitStack() as ctx:
        keep = ctx.enter_context(tc.tile_pool(name="keep", bufs=1))
        work = ctx.enter_context(tc.tile_pool(name="work", bufs=3))
        psum = ctx.enter_context(tc.psum_pool(name="psum", bufs=1))
        results = ctx.enter_context(tc.tile_pool(name="results", bufs=8))
        ctx.enter_context(tc.manual_schedule())

        ident = keep.tile([P, P], F32, name="ident")
        make_identity(nc, ident[:])

        phi_plane = [keep.tile([P, PASSES, HALF], U8, name="phi_plane%d" % h, align_bytes=64) for h in range(2)]
        grad_plane = keep.tile([P, PASSES, N], U8, name="grad_plane", align_bytes=64)
        for plane in (phi_plane[0], grad_plane, phi_plane[1]):
            nc.vector.memset(plane[:].rearrange("p g n -> p (g n)").bitcast(I32), 0)

        def load_scales(plane, rows, cols):
            by_row = rows.rearrange("g (q r) n -> r q g n", r=4)
            for r in range(4):
                nc.sync.dma_start(out=plane[r:P:32, :, :].bitcast(I32), in_=by_row[r][:, :, cols].bitcast(I32))

        amp_sb, res_sb, phi_sb, grad_sb, delta_sb = {}, {}, {}, {}, {}

        def load_x(i):
            amp_sb[i] = keep.tile([P, K], BF16, name="amp%d" % i)
            res_sb[i] = keep.tile([P, K], BF16, name="res%d" % i)
            nc.sync.dma_start(out=amp_sb[i][:], in_=amp[i * P : (i + 1) * P, :])
            nc.sync.dma_start(out=res_sb[i][:], in_=res[i * P : (i + 1) * P, :])

        def load_phi(h):
            phi_sb[h] = keep.tile([P, PASSES, 2 * HALF], U8, name="phi%d" % h, align_bytes=64)
            src = phi_words.rearrange("g p b -> p g b")[:, :, 2 * HALF * h : 2 * HALF * (h + 1)]
            nc.sync.dma_start(out=phi_sb[h][:].bitcast(I32), in_=src.bitcast(I32))

        def load_grad(h):
            for g in range(PASSES):
                grad_sb[h, g] = keep.tile([P, HALF], U32, name="grad%d%d" % (h, g), align_bytes=64)
                src = grad_words[g].rearrange("p n t -> p (n t)")[:, PACK * HALF * h : PACK * HALF * (h + 1)]
                nc.sync.dma_start(out=grad_sb[h, g][:].bitcast(I32), in_=src.bitcast(I32))

        def load_delta(h, g):
            delta_sb[h, g] = keep.tile([P, PACK, HALF], BF16, name="delta%d%d" % (h, g))
            rows = delta[P * PACK * g : P * PACK * (g + 1), HALF * h : HALF * (h + 1)]
            nc.sync.dma_start(out=delta_sb[h, g][:], in_=rows.rearrange("(p t) n -> p t n", t=PACK))

        pattern_rows = keep.tile([P, N // P], BF16, name="pattern_rows")
        nc.sync.dma_start(out=pattern_rows[:], in_=pattern.rearrange("(p c) -> p c", p=P))
        load_x(0)
        load_x(1)
        load_scales(phi_plane[0], phi_scales, slice(0, HALF))
        load_phi(0)
        load_x(2)
        load_scales(grad_plane, grad_scales, slice(0, N))
        load_grad(0)
        load_x(3)
        load_grad(1)
        load_delta(0, 0)
        load_delta(0, 1)
        load_x(4)
        load_delta(0, 2)
        load_x(5)
        load_delta(1, 0)
        load_x(6)
        load_delta(1, 1)
        load_x(7)
        load_delta(1, 2)
        load_scales(phi_plane[1], phi_scales, slice(HALF, N))
        load_phi(1)

        pattern_sb = keep.tile([P, N], BF16, name="pattern_sb")
        pattern_words = pattern_rows[:].bitcast(F32)
        spread = psum.tile([P, 4, P], F32, name="spread", tag="turn_a")
        for c in range(4):
            nc.tensor.transpose(spread[:, c, :], pattern_words[:, c : c + 1].to_broadcast([P, P]), ident[:])
        nc.scalar.copy(
            out=pattern_sb[:].bitcast(F32).rearrange("q (p c) -> q p c", c=4),
            in_=spread[:].rearrange("q c p -> q p c"),
        )

        x_sorted, x_codes, x_plane, d_codes, d_plane = {}, {}, {}, {}, {}
        x_grouped, d_grouped, u_sb, p_bank, weighted = {}, {}, {}, {}, {}
        free_banks = list(range(6))

        def multiply(i):
            x_sorted[i] = work.tile([P, K], BF16, name="x_sorted")
            nc.vector.tensor_tensor(
                out=x_sorted[i][:].rearrange("m (u w e) -> m u w e", u=2, e=2),
                in0=amp_sb[i][:].rearrange("m (w u e) -> m u w e", u=2, e=2),
                in1=res_sb[i][:].rearrange("m (w u e) -> m u w e", u=2, e=2),
                op=MULT,
            )

        def turn(i):
            words = x_sorted[i][:].bitcast(F32)
            bank_a = psum.tile([P, 4, P], F32, name="bank_a", tag="turn_a")
            bank_b = psum.tile([P, 2, P], F32, name="bank_b", tag="turn_b")
            for g in range(PASSES):
                for u in range(2):
                    dst = bank_a[:, 2 * g + u, :] if g < 2 else bank_b[:, u, :]
                    first = u * (K // 4) + g * P
                    nc.tensor.transpose(dst, words[:, first : first + P], ident[:])
            grouped_a = work.tile([P, 1024], BF16, name="grouped_a", align_bytes=64)
            grouped_b = work.tile([P, 512], BF16, name="grouped_b", align_bytes=64)
            nc.scalar.copy(
                out=grouped_a[:].bitcast(F32).rearrange("p (g m u) -> p g m u", g=2, u=2),
                in_=bank_a[:].rearrange("p (g u) m -> p g m u", g=2),
            )
            nc.scalar.copy(
                out=grouped_b[:].bitcast(F32).rearrange("p (m u) -> p m u", u=2),
                in_=bank_b[:].rearrange("p u m -> p m u"),
            )
            x_grouped[i] = (grouped_a, grouped_b)

        def quantize_x(i):
            grouped_a, grouped_b = x_grouped[i]
            x_codes[i] = keep.tile([P, PASSES * P], U32, name="x_codes%d" % i, align_bytes=64)
            x_plane[i] = keep.tile([P, PASSES * P], U8, name="x_plane%d" % i, align_bytes=64)
            nc.vector.quantize_mx(
                out=x_codes[i][:, : 2 * P].bitcast(FP8X4), scales=x_plane[i][:, : 2 * P], in_=grouped_a[:]
            )
            nc.vector.quantize_mx(
                out=x_codes[i][:, 2 * P :].bitcast(FP8X4), scales=x_plane[i][:, 2 * P :], in_=grouped_b[:]
            )

        def regroup(h, g, first, last, on_vector):
            if (h, g) not in d_grouped:
                d_grouped[h, g] = work.tile([P, HALF * PACK], BF16, name="delta_grouped", align_bytes=64)
            dst = d_grouped[h, g][:, PACK * PIECE * first : PACK * PIECE * last]
            src = delta_sb[h, g][:, :, PIECE * first : PIECE * last]
            dst = dst.rearrange("p (c i t) -> p c t i", i=4, t=PACK)
            src = src.rearrange("p t (c i) -> p c t i", i=4)
            if on_vector:
                nc.vector.tensor_copy(out=dst, in_=src)
            else:
                nc.scalar.copy(out=dst, in_=src)

        def quantize_delta(h, g):
            d_codes[h, g] = keep.tile([P, HALF], U32, name="d_codes%d%d" % (h, g), align_bytes=64)
            d_plane[h, g] = keep.tile([P, HALF], U8, name="d_plane%d%d" % (h, g), align_bytes=64)
            nc.vector.quantize_mx(out=d_codes[h, g][:].bitcast(FP8X4), scales=d_plane[h, g][:], in_=d_grouped[h, g][:])

        def mx_pass(bank, i, g, rhs, rhs_scale, start, stop):
            nc.tensor.matmul_mx(
                out=bank[:],
                lhsT=x_codes[i][:, g * P : (g + 1) * P].bitcast(FP8X4),
                lhsT_scale=x_plane[i][:, g * P : (g + 1) * P],
                rhs=rhs,
                rhs_scale=rhs_scale,
                start=start,
                stop=stop,
            )

        def velocity(i, h):
            number = free_banks.pop(0)
            bank = psum.tile([P, HALF], F32, name="sum%d" % number)
            for g in range(PASSES):
                scale = grad_plane[:, g, HALF * h : HALF * (h + 1)]
                mx_pass(bank, i, g, grad_sb[h, g][:].bitcast(FP8X4), scale, g == 0, g == PASSES - 1)
            if h == 0:
                u_sb[i, h] = results.tile([P, HALF], F32, name="u_first", bufs=5)
            else:
                u_sb[i, h] = results.tile([P, HALF], F32, name="u_second")
            nc.scalar.copy(out=u_sb[i, h][:], in_=bank[:])
            free_banks.append(number)

        def base(i, h):
            number = free_banks.pop(0)
            bank = psum.tile([P, HALF], F32, name="sum%d" % number)
            p_bank[i, h] = (number, bank)
            for g in range(PASSES):
                scale = phi_plane[h][:, g, :]
                mx_pass(bank, i, g, phi_sb[h][:, g, :].bitcast(FP4X4), scale, g == 0, False)

        def correction(tiles, h, passes):
            for g in passes:
                for i in tiles:
                    rhs = d_codes[h, g][:].bitcast(FP8X4)
                    mx_pass(p_bank[i, h][1], i, g, rhs, d_plane[h, g][:], False, g == PASSES - 1)

        def weigh(i, h):
            weighted[i, h] = results.tile([P, HALF], F32, name="signal", bufs=5)
            engine = nc.vector if h == 0 else nc.gpsimd
            engine.tensor_tensor(
                out=weighted[i, h][:], in0=u_sb[i, h][:], in1=pattern_sb[:, HALF * h : HALF * (h + 1)], op=MULT
            )

        def finish(i, h):
            cols = slice(HALF * h, HALF * (h + 1))
            rows = slice(P * i, P * (i + 1))
            number, bank = p_bank[i, h]
            intensity = results.tile([P, HALF], F32, name="intensity")
            signal = weighted[i, h]
            nc.vector.tensor_tensor(out=intensity[:], in0=bank[:], in1=u_sb[i, h][:], op=MULT)
            nc.vector.tensor_tensor(out=signal[:], in0=bank[:], in1=signal[:], op=ADD)
            free_banks.append(number)
            nc.sync.dma_start(out=out_1[rows, cols], in_=intensity[:])
            nc.sync.dma_start(out=out_0[rows, cols], in_=signal[:])

        def pressure(i, h):
            base(i, h)
            correction([i], h, range(PASSES))

        def last_pressure(i, h):
            rows = slice(P * i, P * (i + 1))
            intensity = results.tile([P, HALF], F32, name="intensity")
            signal = weighted[i, h]
            for j in range(HALF // P):
                part = slice(P * j, P * (j + 1))
                number = free_banks.pop(0)
                bank = psum.tile([P, P], F32, name="sum%d" % number)
                for g in range(PASSES):
                    scale = phi_plane[h][:, g, part]
                    rhs = phi_sb[h][:, g, 2 * P * j : 2 * P * (j + 1)].bitcast(FP4X4)
                    mx_pass(bank, i, g, rhs, scale, g == 0, False)
                for g in range(PASSES):
                    rhs = d_codes[h, g][:, part].bitcast(FP8X4)
                    mx_pass(bank, i, g, rhs, d_plane[h, g][:, part], False, g == PASSES - 1)
                nc.vector.tensor_tensor(out=intensity[:, part], in0=bank[:], in1=u_sb[i, h][:, part], op=MULT)
                nc.vector.tensor_tensor(out=signal[:, part], in0=bank[:], in1=signal[:, part], op=ADD)
                free_banks.append(number)
                if j >= 2:
                    first = 0 if j == 2 else P * j
                    done = slice(first, P * (j + 1))
                    cols = slice(HALF * h + first, HALF * h + P * (j + 1))
                    nc.sync.dma_start(out=out_1[rows, cols], in_=intensity[:, done])
                    nc.sync.dma_start(out=out_0[rows, cols], in_=signal[:, done])

        multiply(0)
        turn(0)
        multiply(1)
        quantize_x(0)
        turn(1)
        base(0, 0)
        quantize_x(1)
        multiply(2)
        base(1, 0)
        turn(2)
        velocity(0, 0)
        quantize_x(2)
        velocity(1, 0)
        multiply(3)
        base(2, 0)
        weigh(0, 0)
        velocity(2, 0)
        turn(3)
        weigh(1, 0)
        weigh(2, 0)
        velocity(0, 1)
        quantize_x(3)
        velocity(1, 1)
        regroup(0, 0, 0, 4, True)
        regroup(0, 1, 3, 4, False)
        velocity(2, 1)
        regroup(0, 1, 0, 3, True)
        quantize_delta(0, 0)
        base(3, 0)
        multiply(4)
        quantize_delta(0, 1)
        velocity(3, 0)
        regroup(0, 2, 3, 4, False)
        regroup(0, 2, 0, 3, True)
        velocity(3, 1)
        quantize_delta(0, 2)
        correction(range(4), 0, [0])
        turn(4)
        quantize_x(4)
        multiply(5)
        correction(range(4), 0, [1, 2])
        finish(0, 0)
        regroup(1, 0, 0, 3, False)
        finish(1, 0)
        finish(2, 0)
        for i in range(4, TILES):
            step = i - 4
            velocity(i, 0)
            if i + 1 < TILES:
                turn(i + 1)
                quantize_x(i + 1)
            if i + 2 < TILES:
                multiply(i + 2)
            if step == 0:
                regroup(1, 0, 3, 4, False)
                weigh(3, 0)
            regroup(1, 1 + step // 2, 2 * (step % 2), 2 * (step % 2) + 2, False)
            if step > 0:
                quantize_delta(1, step - 1)
            finish(i - 1, 0)
            weigh(i, 0)
            pressure(i, 0)
            velocity(i, 1)
        finish(TILES - 1, 0)
        weigh(0, 1)
        for i in range(TILES - 1):
            pressure(i, 1)
            weigh(i + 1, 1)
            finish(i, 1)
        last_pressure(TILES - 1, 1)
